import numpy as np
import ml_dtypes


def mxq(x, axis, fmt="e4m3"):
    dtype, down = {"e4m3": (ml_dtypes.float8_e4m3fn, 7), "e5m2": (ml_dtypes.float8_e5m2, 14)}[fmt]
    v = np.moveaxis(np.asarray(x, np.float32).astype(ml_dtypes.bfloat16).astype(np.float64), axis, -1)
    blocks = v.reshape(v.shape[:-1] + (-1, 32))
    amax = np.abs(blocks).max(-1, keepdims=True)
    byte = np.maximum(np.where(amax > 0, np.frexp(amax)[1] - 1 + 127, 0) - down, 1)
    scale = np.exp2(byte - 127.0)
    codes = (blocks / scale).astype(np.float32).astype(dtype).astype(np.float64)
    return np.moveaxis((codes * scale).reshape(v.shape), -1, axis)


WIDE = False


def mx_kscale(k):
    if not WIDE:
        return np.ones(k)
    levels = np.array([30, -30])
    if k % 512:
        return np.exp2(np.random.permutation(np.resize(levels, k // 32))).repeat(32)
    a = np.empty((k // 512, 16))
    for p in range(k // 512):
        a[p, :8] = np.random.permutation(np.resize(levels, 8))
        for g in range(8):
            far = levels[np.abs(levels - a[p, g]) >= 10]
            a[p, g + 8] = far[np.random.randint(len(far))]
    return np.exp2(a.ravel()).repeat(32)


def f64(x):
    return np.asarray(x).astype(np.float64)


def striped(idx):
    return np.tile(np.asarray(idx).reshape(-1, 16).T, (8, 1)).astype(np.uint16)


def unstriped(offs):
    return offs[:16].T.reshape(-1).astype(np.int64)


E2M1 = np.array([0.0, 0.5, 1.0, 1.5, 2.0, 3.0, 4.0, 6.0, -0.0, -0.5, -1.0, -1.5, -2.0, -3.0, -4.0, -6.0])


def pack_weight(w, fmt):
    k, n = w.shape
    w = f64(np.asarray(w, np.float32).astype(ml_dtypes.bfloat16)).reshape(k // 32, 32, n)
    amax = np.abs(w).max(1)
    if fmt in ("e4m3", "e5m2"):
        byte = np.frexp(amax)[1] - 1 + 127 - (7 if fmt == "e4m3" else 14)
    else:
        mant, ex = np.frexp(amax / 6.0)
        byte = np.where(mant > 0.5, ex, ex - 1) + 127
    byte = np.clip(np.where(amax > 0, byte, 1), 1, 254)
    scaled = (w * np.exp2(127.0 - byte)[:, None, :]).reshape(k, n).astype(np.float32)
    by_word = np.ascontiguousarray(scaled.reshape(k // 512, 128, 4, n).transpose(0, 1, 3, 2))
    if fmt in ("e4m3", "e5m2"):
        words = by_word.astype(ml_dtypes.float8_e4m3fn if fmt == "e4m3" else ml_dtypes.float8_e5m2).view(np.uint8)
    else:
        c = by_word.astype(ml_dtypes.float4_e2m1fn).view(np.uint8) & 0xF
        words = (c[..., 0::2] | (c[..., 1::2] << 4)).reshape(k // 512, 128, 2 * n)
    return np.ascontiguousarray(words), np.ascontiguousarray(byte.astype(np.uint8).reshape(k // 512, 16, n))


def unpack_weight(words, scales, fmt):
    g, _, n = scales.shape
    words = np.ascontiguousarray(words).reshape(g, 128, n, -1)
    if fmt in ("e4m3", "e5m2"):
        vals = words.view(ml_dtypes.float8_e4m3fn if fmt == "e4m3" else ml_dtypes.float8_e5m2).astype(np.float64)
    else:
        nib = np.empty((g, 128, n, 4), np.uint8)
        nib[..., 0::2] = words & 0xF
        nib[..., 1::2] = words >> 4
        vals = E2M1[nib]
    vals = vals * np.repeat(np.exp2(scales.astype(np.float64) - 127.0), 8, axis=1)[..., None]
    return vals.transpose(0, 1, 3, 2).reshape(g * 512, n)


K, T, J, S, R, F, Z, N = 512, 512, 256, 512, 512, 512, 1024, 256


def setup_inputs():
    n = np.random.standard_normal
    idx = np.random.permutation(T)[:J]
    idx2 = np.random.permutation(S)[:J]
    idx3 = np.random.permutation(Z)[:J]
    fk = mx_kscale(K)
    fr = mx_kscale(R)
    ff = mx_kscale(F)
    wp = pack_weight(n((K, R)) * 1 / np.sqrt(K) * fk[:, None] * fr, "e5m2")
    xop = pack_weight(n((F, Z)) / ff[:, None], "e4m3")
    w2p = pack_weight(n((F, R)) * 1 / np.sqrt(F) * ff[:, None] * fr, "e5m2")
    wbp = pack_weight(n((R, N)) * 1 / np.sqrt(R) / fr[:, None], "e4m3")
    return {
        "xa": (n((K, T))).astype(np.float32),
        "xb": (n((K, S))).astype(np.float32),
        "hb": (np.random.uniform(0.2, 0.9, (K, 1))).astype(np.float32),
        "fk": (np.random.uniform(0.5, 2.0, (K, 1)) / fk[:, None]).astype(np.float32),
        "w_words": wp[0],
        "w_scales": wp[1],
        "xo_words": xop[0],
        "xo_scales": xop[1],
        "w2_words": w2p[0],
        "w2_scales": w2p[1],
        "wb_words": wbp[0],
        "wb_scales": wbp[1],
        "rs": (1.0 * n((J, N))).astype(np.float32),
        "offs": striped(idx),
        "offs2": striped(idx2),
        "offs3": striped(idx3),
    }


def reference(xa, xb, hb, fk, w_words, w_scales, xo_words, xo_scales, w2_words, w2_scales, wb_words, wb_scales, rs, offs, offs2, offs3):
    idx = unstriped(offs)
    idx2 = unstriped(offs2)
    idx3 = unstriped(offs3)
    wu = unpack_weight(w_words, w_scales, "e5m2")
    xou = unpack_weight(xo_words, xo_scales, "e4m3")
    w2u = unpack_weight(w2_words, w2_scales, "e5m2")
    wbu = unpack_weight(wb_words, wb_scales, "e4m3")
    u = (f64(xa)[:, idx] - np.minimum(f64(xb)[:, idx2], f64(hb))) * f64(fk)
    uq = mxq(u, 0, "e5m2")
    a = wu.T @ uq
    xoidx3g = xou[:, idx3]
    q = w2u.T @ xoidx3g
    y1 = np.pad(q, ((0, 0), (1, 0)))[:, :J]
    hid = np.maximum(a, q - 0.6 * y1)
    hidq = mxq(hid, 0, "e5m2")
    p = hidq.T @ wbu
    pk2 = np.max(np.abs(p), axis=1, keepdims=True)
    y = p / (pk2 + 0.2) + 0.3 * f64(rs)
    return y

@@ -1,0 +1,214 @@
+from contextlib import ExitStack
+
+import concourse.mybir as mybir
+
+K, T, J, S, R, F, Z, N = 512, 512, 256, 512, 512, 512, 1024, 256
+FLOPS = 2 * J * (K * R + F * R + R * N)
+
+F32 = mybir.dt.float32
+BF16 = mybir.dt.bfloat16
+I32 = mybir.dt.int32
+U32 = mybir.dt.uint32
+U16 = mybir.dt.uint16
+U8 = mybir.dt.uint8
+E4M3 = mybir.dt.float8_e4m3fn_x4
+E5M2 = mybir.dt.float8_e5m2_x4
+ALU = mybir.AluOpType
+ACT = mybir.ActivationFunctionType
+
+P = 128
+PACK = 4
+H = 128
+HALVES = J // H
+LINE = 4
+
+
+def tile_list_two_boundedgaps_other_stepgap_rowpeaks_kernel(
+    tc, xa, xb, hb, fk, w_words, w_scales, xo_words, xo_scales, w2_words, w2_scales,
+    wb_words, wb_scales, rs, offs, offs2, offs3, out,
+):
+    nc = tc.nc
+    with ExitStack() as ctx:
+        sb = ctx.enter_context(tc.tile_pool(name="sb", bufs=1))
+        ps = ctx.enter_context(tc.psum_pool(name="ps", bufs=1))
+
+        def tile(shape, dtype, name):
+            return sb.tile(shape, dtype, name=name, align_bytes=64)
+
+        list_a = tile([P, J // 16], U16, "list_a")
+        list_b = tile([P, J // 16], U16, "list_b")
+        list_o = tile([P, J // 16], U16, "list_o")
+        xa_sb = [tile([P, T], F32, "xa_sb%d" % t) for t in range(PACK)]
+        xb_sb = [tile([P, S], F32, "xb_sb%d" % t) for t in range(PACK)]
+        hb_sb = tile([P, PACK], F32, "hb_sb")
+        fk_sb = tile([P, PACK], F32, "fk_sb")
+        xo_w = tile([P, Z], U32, "xo_w")
+        xo_s = tile([P, Z], U8, "xo_s")
+        w_w = tile([P, R], U32, "w_w")
+        w_s = tile([P, R], U8, "w_s")
+        w2_w = tile([P, R], U32, "w2_w")
+        w2_s = tile([P, R], U8, "w2_s")
+        wb_w = tile([P, N], U32, "wb_w")
+        wb_s = tile([P, N], U8, "wb_s")
+        rs_sb = tile([P, HALVES, N], F32, "rs_sb")
+        q_sb = tile([P, J + 1, PACK], F32, "q_sb")
+
+        for plane in (xo_s, w2_s, w_s, wb_s):
+            nc.vector.memset(plane[:].bitcast(I32), 0)
+        nc.vector.memset(q_sb[:, 0, :], 0.0)
+
+        xa_rows = xa.rearrange("(p t) c -> t p c", t=PACK)
+        xb_rows = xb.rearrange("(p t) c -> t p c", t=PACK)
+
+        def load_words(dst, src):
+            nc.sync.dma_start(out=dst[:].bitcast(I32), in_=src[0].rearrange("p n t -> p (n t)").bitcast(I32))
+
+        def load_scales(queue, dst, src, quad):
+            queue.dma_start(
+                out=dst[32 * quad : 32 * quad + 4, :].bitcast(I32),
+                in_=src[0, 4 * quad : 4 * quad + 4, :].bitcast(I32),
+            )
+
+        nc.sync.dma_start(list_b[:], offs2)
+        nc.sync.dma_start(out=xb_sb[0][:], in_=xb_rows[0])
+        nc.sync.dma_start(list_o[:], offs3)
+        load_words(xo_w, xo_words)
+        for quad in range(4):
+            load_scales(nc.sync, xo_s, xo_scales, quad)
+        nc.sync.dma_start(list_a[:], offs)
+        nc.sync.dma_start(out=xa_sb[0][:], in_=xa_rows[0])
+        load_words(w2_w, w2_words)
+        nc.sync.dma_start(out=xb_sb[1][:], in_=xb_rows[1])
+        for quad in range(4):
+            load_scales(nc.sync, w2_s, w2_scales, quad)
+        nc.sync.dma_start(out=xa_sb[1][:], in_=xa_rows[1])
+        nc.sync.dma_start(out=xb_sb[2][:], in_=xb_rows[2])
+        nc.sync.dma_start(out=xa_sb[2][:], in_=xa_rows[2])
+        nc.sync.dma_start(out=xb_sb[3][:], in_=xb_rows[3])
+        nc.sync.dma_start(out=xa_sb[3][:], in_=xa_rows[3])
+        for quad in range(4):
+            load_scales(nc.sync, w_s, w_scales, quad)
+        load_words(w_w, w_words)
+        load_words(wb_w, wb_words)
+        nc.sync.dma_start(out=rs_sb[:], in_=rs.rearrange("(h p) n -> p h n", p=P))
+        for quad in range(4):
+            load_scales(nc.sync, wb_s, wb_scales, quad)
+        nc.gpsimd.dma_start(out=hb_sb[:], in_=hb.rearrange("(p t) o -> p (t o)", t=PACK))
+        nc.gpsimd.dma_start(out=fk_sb[:], in_=fk.rearrange("(p t) o -> p (t o)", t=PACK))
+
+        def deal(words, scales, name, on_scalar):
+            dealt_w = tile([P, PACK, P], U32, name + "_dw")
+            dealt_s = tile([P, PACK, P], U8, name + "_ds")
+            if on_scalar:
+                nc.scalar.copy(
+                    out=dealt_w[:].rearrange("p t (c i) -> p c t i", i=LINE),
+                    in_=words[:].rearrange("p (c i t) -> p c t i", i=LINE, t=PACK),
+                )
+            else:
+                nc.vector.tensor_copy(
+                    out=dealt_w[:].bitcast(I32).rearrange("p t (c i) -> p c t i", i=LINE),
+                    in_=words[:].bitcast(I32).rearrange("p (c i t) -> p c t i", i=LINE, t=PACK),
+                )
+            nc.vector.tensor_copy(out=dealt_s[:], in_=scales[:].rearrange("p (m t) -> p t m", t=PACK))
+            return dealt_w, dealt_s
+
+        xa_g = [tile([P, J], F32, "xa_g%d" % t) for t in range(PACK)]
+        xb_g = [tile([P, J], F32, "xb_g%d" % t) for t in range(PACK)]
+        gap = tile([P, PACK, J], F32, "gap")
+
+        def plane_gap(t):
+            nc.scalar.activation(out=xb_g[t][:], in_=xb_sb[t][:].indirect(list_b[:]), func=ACT.Copy)
+            if t < PACK // 2:
+                nc.scalar.activation(out=xa_g[t][:], in_=xa_sb[t][:].indirect(list_a[:]), func=ACT.Copy)
+            else:
+                nc.vector.tensor_copy(out=xa_g[t][:], in_=xa_sb[t][:].indirect(list_a[:]))
+            nc.vector.scalar_tensor_tensor(
+                out=gap[:, t, :], in0=xb_g[t][:], scalar=hb_sb[:, t : t + 1], in1=xa_g[t][:],
+                op0=ALU.min, op1=ALU.subtract,
+            )
+
+        xo_gw = tile([P, J], U32, "xo_gw")
+        xo_gs = tile([P, J], U8, "xo_gs")
+        nc.vector.tensor_copy(out=xo_gw[:], in_=xo_w[:].indirect(list_o[:]))
+        nc.vector.tensor_copy(out=xo_gs[:], in_=xo_s[:].indirect(list_o[:]))
+        w2_dw, w2_ds = deal(w2_w, w2_s, "w2", False)
+        plane_gap(0)
+
+        step = [tile([P, H * PACK], F32, "step%d" % h) for h in range(HALVES)]
+        q_ps = [ps.tile([P, PACK, H], F32, name="q_ps%d" % h) for h in range(HALVES)]
+        for h in range(HALVES):
+            cols = slice(h * H, (h + 1) * H)
+            for t in range(PACK):
+                nc.tensor.matmul_mx(
+                    out=q_ps[h][:, t, :], lhsT=w2_dw[:, t, :].bitcast(E5M2), lhsT_scale=w2_ds[:, t, :],
+                    rhs=xo_gw[:, cols].bitcast(E4M3), rhs_scale=xo_gs[:, cols], start=True, stop=True,
+                )
+        plane_gap(1)
+        plane_gap(2)
+        neg_fk = tile([P, PACK], F32, "neg_fk")
+        nc.gpsimd.tensor_scalar(out=neg_fk[:], in0=fk_sb[:], scalar1=-1.0, scalar2=0.0, op0=ALU.mult, op1=ALU.add)
+        plane_gap(3)
+        for h in range(HALVES):
+            nc.scalar.copy(out=q_sb[:, 1 + h * H : 1 + (h + 1) * H, :], in_=q_ps[h][:].rearrange("p t j -> p j t"))
+            nc.vector.scalar_tensor_tensor(
+                out=step[h][:],
+                in0=q_sb[:, h * H : (h + 1) * H, :].rearrange("p j t -> p (j t)"),
+                scalar=-0.6,
+                in1=q_sb[:, 1 + h * H : 1 + (h + 1) * H, :].rearrange("p j t -> p (j t)"),
+                op0=ALU.mult, op1=ALU.add,
+            )
+
+
+        factor = neg_fk[:].rearrange("p (c t i) -> p c t i", c=1, i=1).to_broadcast([P, H // LINE, PACK, LINE])
+        u_bf, u_w, u_s = [], [], []
+        for h in range(HALVES):
+            u_bf.append(tile([P, H, PACK], BF16, "u_bf%d" % h))
+            nc.vector.tensor_tensor(
+                out=u_bf[h][:].rearrange("p (c i) t -> p c t i", i=LINE),
+                in0=gap[:, :, h * H : (h + 1) * H].rearrange("p t (c i) -> p c t i", i=LINE),
+                in1=factor, op=ALU.mult,
+            )
+        w_dw, w_ds = deal(w_w, w_s, "w", True)
+        rs3 = tile([P, HALVES, N], F32, "rs3")
+        nc.scalar.activation(out=rs3[:], in_=rs_sb[:], func=ACT.Copy, scale=0.3)
+        a_ps = []
+        for h in range(HALVES):
+            u_w.append(tile([P, H], U32, "u_w%d" % h))
+            u_s.append(tile([P, H], U8, "u_s%d" % h))
+            nc.vector.quantize_mx(out=u_w[h][:].bitcast(E5M2), scales=u_s[h][:], in_=u_bf[h][:].rearrange("p j t -> p (j t)"))
+            a_ps.append(ps.tile([P, PACK, H], F32, name="a_ps%d" % h))
+            for t in range(PACK):
+                nc.tensor.matmul_mx(
+                    out=a_ps[h][:, t, :], lhsT=w_dw[:, t, :].bitcast(E5M2), lhsT_scale=w_ds[:, t, :],
+                    rhs=u_w[h][:].bitcast(E5M2), rhs_scale=u_s[h][:], start=True, stop=True,
+                )
+        hid_bf, p_ps = [], []
+        for h in range(HALVES):
+            hid_bf.append(tile([P, H, PACK], BF16, "hid_bf%d" % h))
+            nc.vector.tensor_tensor(
+                out=hid_bf[h][:], in0=a_ps[h][:].rearrange("p t j -> p j t"),
+                in1=step[h][:].rearrange("p (j t) -> p j t", t=PACK), op=ALU.max,
+            )
+        for h in range(HALVES):
+            hid_w = tile([P, H], U32, "hid_w%d" % h)
+            hid_s = tile([P, H], U8, "hid_s%d" % h)
+            nc.vector.quantize_mx(out=hid_w[:].bitcast(E5M2), scales=hid_s[:], in_=hid_bf[h][:].rearrange("p j t -> p (j t)"))
+            p_ps.append(ps.tile([P, N], F32, name="p_ps%d" % h))
+            nc.tensor.matmul_mx(
+                out=p_ps[h][:], lhsT=hid_w[:].bitcast(E5M2), lhsT_scale=hid_s[:],
+                rhs=wb_w[:].bitcast(E4M3), rhs_scale=wb_s[:], start=True, stop=True,
+            )
+        for h in range(HALVES):
+            size = tile([P, N], F32, "size%d" % h)
+            peak = tile([P, 1], F32, "peak%d" % h)
+            inv = tile([P, 1], F32, "inv%d" % h)
+            res = tile([P, N], F32, "res%d" % h)
+            nc.scalar.activation(out=size[:], in_=p_ps[h][:], func=ACT.Abs)
+            nc.vector.tensor_scalar(
+                out=size[:], in0=size[:], scalar1=0.2, scalar2=None, op0=ALU.add, op1=ALU.max, accum_out=peak[:],
+            )
+            nc.vector.reciprocal(out=inv[:], in_=peak[:])
+            nc.vector.scalar_tensor_tensor(
+                out=res[:], in0=p_ps[h][:], scalar=inv[:], in1=rs3[:, h, :], op0=ALU.mult, op1=ALU.add,
+            )
+            nc.sync.dma_start(out=out[h * H : (h + 1) * H, :], in_=res[:])

@@ -32,33 +32,34 @@ def tile_list_two_boundedgaps_other_stepgap_rowpeaks_kernel(
         sb = ctx.enter_context(tc.tile_pool(name="sb", bufs=1))
         ps = ctx.enter_context(tc.psum_pool(name="ps", bufs=1))
 
-        def tile(shape, dtype, name):
-            return sb.tile(shape, dtype, name=name, align_bytes=64)
+        def tile(shape, dtype, name, tag=None):
+            return sb.tile(shape, dtype, name=name, tag=tag or name, align_bytes=64)
 
         list_a = tile([P, J // 16], U16, "list_a")
         list_b = tile([P, J // 16], U16, "list_b")
         list_o = tile([P, J // 16], U16, "list_o")
-        xa_sb = [tile([P, T], F32, "xa_sb%d" % t) for t in range(PACK)]
-        xb_sb = [tile([P, S], F32, "xb_sb%d" % t) for t in range(PACK)]
+        xa_sb = [tile([P, 2, T], F32, "xa_sb%d" % g) for g in range(2)]
+        xb_sb = [tile([P, 2, S], F32, "xb_sb%d" % g) for g in range(2)]
         hb_sb = tile([P, PACK], F32, "hb_sb")
         fk_sb = tile([P, PACK], F32, "fk_sb")
         xo_w = tile([P, Z], U32, "xo_w")
         xo_s = tile([P, Z], U8, "xo_s")
         w_w = tile([P, R], U32, "w_w")
-        w_s = tile([P, R], U8, "w_s")
         w2_w = tile([P, R], U32, "w2_w")
-        w2_s = tile([P, R], U8, "w2_s")
         wb_w = tile([P, N], U32, "wb_w")
-        wb_s = tile([P, N], U8, "wb_s")
+        planes = tile([P, 2 * R + N], U8, "planes")
+        w2_s, w_s, wb_s = planes[:, 0:R], planes[:, R : 2 * R], planes[:, 2 * R : 2 * R + N]
         rs_sb = tile([P, HALVES, N], F32, "rs_sb")
         q_sb = tile([P, J + 1, PACK], F32, "q_sb")
 
-        for plane in (xo_s, w2_s, w_s, wb_s):
-            nc.vector.memset(plane[:].bitcast(I32), 0)
-        nc.vector.memset(q_sb[:, 0, :], 0.0)
+        nc.vector.memset(xo_s[:].bitcast(I32), 0)
+        nc.gpsimd.memset(planes[:].bitcast(I32), 0)
+        zeros = tile([P, PACK], F32, "zeros")
+        nc.vector.memset(zeros[:], 0.0)
+        nc.scalar.activation(out=q_sb[:, 0, :], in_=zeros[:], func=ACT.Copy)
 
-        xa_rows = xa.rearrange("(p t) c -> t p c", t=PACK)
-        xb_rows = xb.rearrange("(p t) c -> t p c", t=PACK)
+        xa_rows = xa.rearrange("(p g e) c -> g p e c", g=2, e=2)
+        xb_rows = xb.rearrange("(p g e) c -> g p e c", g=2, e=2)
 
         def load_words(dst, src):
             nc.sync.dma_start(out=dst[:].bitcast(I32), in_=src[0].rearrange("p n t -> p (n t)").bitcast(I32))
@@ -69,25 +70,21 @@ def tile_list_two_boundedgaps_other_stepgap_rowpeaks_kernel(
                 in_=src[0, 4 * quad : 4 * quad + 4, :].bitcast(I32),
             )
 
-        nc.sync.dma_start(list_b[:], offs2)
-        nc.sync.dma_start(out=xb_sb[0][:], in_=xb_rows[0])
         nc.sync.dma_start(list_o[:], offs3)
+        nc.sync.dma_start(list_b[:], offs2)
         load_words(xo_w, xo_words)
         for quad in range(4):
             load_scales(nc.sync, xo_s, xo_scales, quad)
-        nc.sync.dma_start(list_a[:], offs)
-        nc.sync.dma_start(out=xa_sb[0][:], in_=xa_rows[0])
+        nc.sync.dma_start(out=xb_sb[0][:], in_=xb_rows[0])
         load_words(w2_w, w2_words)
-        nc.sync.dma_start(out=xb_sb[1][:], in_=xb_rows[1])
         for quad in range(4):
             load_scales(nc.sync, w2_s, w2_scales, quad)
-        nc.sync.dma_start(out=xa_sb[1][:], in_=xa_rows[1])
-        nc.sync.dma_start(out=xb_sb[2][:], in_=xb_rows[2])
-        nc.sync.dma_start(out=xa_sb[2][:], in_=xa_rows[2])
-        nc.sync.dma_start(out=xb_sb[3][:], in_=xb_rows[3])
-        nc.sync.dma_start(out=xa_sb[3][:], in_=xa_rows[3])
+        nc.sync.dma_start(list_a[:], offs)
+        nc.sync.dma_start(out=xb_sb[1][:], in_=xb_rows[1])
+        nc.sync.dma_start(out=xa_sb[0][:], in_=xa_rows[0])
         for quad in range(4):
             load_scales(nc.sync, w_s, w_scales, quad)
+        nc.sync.dma_start(out=xa_sb[1][:], in_=xa_rows[1])
         load_words(w_w, w_words)
         load_words(wb_w, wb_words)
         nc.sync.dma_start(out=rs_sb[:], in_=rs.rearrange("(h p) n -> p h n", p=P))
@@ -96,32 +93,39 @@ def tile_list_two_boundedgaps_other_stepgap_rowpeaks_kernel(
         nc.gpsimd.dma_start(out=hb_sb[:], in_=hb.rearrange("(p t) o -> p (t o)", t=PACK))
         nc.gpsimd.dma_start(out=fk_sb[:], in_=fk.rearrange("(p t) o -> p (t o)", t=PACK))
 
-        def deal(words, scales, name, on_scalar):
-            dealt_w = tile([P, PACK, P], U32, name + "_dw")
-            dealt_s = tile([P, PACK, P], U8, name + "_ds")
+        def deal_words(words, name, on_scalar, tag=None):
+            dealt = tile([P, PACK, P], U32, name, tag)
             if on_scalar:
                 nc.scalar.copy(
-                    out=dealt_w[:].rearrange("p t (c i) -> p c t i", i=LINE),
+                    out=dealt[:].rearrange("p t (c i) -> p c t i", i=LINE),
                     in_=words[:].rearrange("p (c i t) -> p c t i", i=LINE, t=PACK),
                 )
             else:
                 nc.vector.tensor_copy(
-                    out=dealt_w[:].bitcast(I32).rearrange("p t (c i) -> p c t i", i=LINE),
+                    out=dealt[:].bitcast(I32).rearrange("p t (c i) -> p c t i", i=LINE),
                     in_=words[:].bitcast(I32).rearrange("p (c i t) -> p c t i", i=LINE, t=PACK),
                 )
-            nc.vector.tensor_copy(out=dealt_s[:], in_=scales[:].rearrange("p (m t) -> p t m", t=PACK))
-            return dealt_w, dealt_s
+            return dealt
 
-        xa_g = [tile([P, J], F32, "xa_g%d" % t) for t in range(PACK)]
+        def deal_scales(scales, name, tag=None):
+            dealt = tile([P, PACK, P], U8, name, tag)
+            nc.vector.tensor_copy(out=dealt[:], in_=scales[:].rearrange("p (m t) -> p t m", t=PACK))
+            return dealt
+
+        xa_g = [tile([P, J], F32, "xa_g%d" % e) for e in range(2)] * 2
         xb_g = [tile([P, J], F32, "xb_g%d" % t) for t in range(PACK)]
         gap = tile([P, PACK, J], F32, "gap")
 
-        def plane_gap(t):
-            nc.scalar.activation(out=xb_g[t][:], in_=xb_sb[t][:].indirect(list_b[:]), func=ACT.Copy)
-            if t < PACK // 2:
-                nc.scalar.activation(out=xa_g[t][:], in_=xa_sb[t][:].indirect(list_a[:]), func=ACT.Copy)
+        def pick_b(t):
+            nc.scalar.activation(out=xb_g[t][:], in_=xb_sb[t // 2][:, t % 2, :].indirect(list_b[:]), func=ACT.Copy)
+
+        def pick_a(t, on_scalar):
+            if on_scalar:
+                nc.scalar.activation(out=xa_g[t][:], in_=xa_sb[t // 2][:, t % 2, :].indirect(list_a[:]), func=ACT.Copy)
             else:
-                nc.vector.tensor_copy(out=xa_g[t][:], in_=xa_sb[t][:].indirect(list_a[:]))
+                nc.vector.tensor_copy(out=xa_g[t][:], in_=xa_sb[t // 2][:, t % 2, :].indirect(list_a[:]))
+
+        def plane_gap(t):
             nc.vector.scalar_tensor_tensor(
                 out=gap[:, t, :], in0=xb_g[t][:], scalar=hb_sb[:, t : t + 1], in1=xa_g[t][:],
                 op0=ALU.min, op1=ALU.subtract,
@@ -131,10 +135,9 @@ def tile_list_two_boundedgaps_other_stepgap_rowpeaks_kernel(
         xo_gs = tile([P, J], U8, "xo_gs")
         nc.vector.tensor_copy(out=xo_gw[:], in_=xo_w[:].indirect(list_o[:]))
         nc.vector.tensor_copy(out=xo_gs[:], in_=xo_s[:].indirect(list_o[:]))
-        w2_dw, w2_ds = deal(w2_w, w2_s, "w2", False)
-        plane_gap(0)
-
-        step = [tile([P, H * PACK], F32, "step%d" % h) for h in range(HALVES)]
+        w2_dw = deal_words(w2_w, "w2_dw", False)
+        w2_ds = deal_scales(w2_s, "w2_ds")
+        step = []
         q_ps = [ps.tile([P, PACK, H], F32, name="q_ps%d" % h) for h in range(HALVES)]
         for h in range(HALVES):
             cols = slice(h * H, (h + 1) * H)
@@ -143,13 +146,12 @@ def tile_list_two_boundedgaps_other_stepgap_rowpeaks_kernel(
                     out=q_ps[h][:, t, :], lhsT=w2_dw[:, t, :].bitcast(E5M2), lhsT_scale=w2_ds[:, t, :],
                     rhs=xo_gw[:, cols].bitcast(E4M3), rhs_scale=xo_gs[:, cols], start=True, stop=True,
                 )
-        plane_gap(1)
-        plane_gap(2)
-        neg_fk = tile([P, PACK], F32, "neg_fk")
-        nc.gpsimd.tensor_scalar(out=neg_fk[:], in0=fk_sb[:], scalar1=-1.0, scalar2=0.0, op0=ALU.mult, op1=ALU.add)
-        plane_gap(3)
-        for h in range(HALVES):
+
+        def copy_q(h):
             nc.scalar.copy(out=q_sb[:, 1 + h * H : 1 + (h + 1) * H, :], in_=q_ps[h][:].rearrange("p t j -> p j t"))
+
+        def make_step(h, tag):
+            step.append(tile([P, H * PACK], F32, "step%d" % h, tag))
             nc.vector.scalar_tensor_tensor(
                 out=step[h][:],
                 in0=q_sb[:, h * H : (h + 1) * H, :].rearrange("p j t -> p (j t)"),
@@ -158,8 +160,27 @@ def tile_list_two_boundedgaps_other_stepgap_rowpeaks_kernel(
                 op0=ALU.mult, op1=ALU.add,
             )
 
+        pick_b(0)
+        pick_b(1)
+        pick_a(0, False)
+        pick_a(1, False)
+        copy_q(0)
+        copy_q(1)
+        neg_fk = tile([P, PACK], F32, "neg_fk", "w2_ds")[:]
+        nc.gpsimd.tensor_scalar(out=neg_fk, in0=fk_sb[:], scalar1=-1.0, scalar2=0.0, op0=ALU.mult, op1=ALU.add)
+        plane_gap(0)
+        plane_gap(1)
+        w_ds = deal_scales(w_s, "w_ds", "xb_g0")
+        make_step(0, "xb_g1")
+        pick_b(2)
+        pick_b(3)
+        pick_a(2, False)
+        pick_a(3, True)
+        plane_gap(2)
+        plane_gap(3)
+        w_dw = deal_words(w_w, "w_dw", True, "xb_g2")
 
-        factor = neg_fk[:].rearrange("p (c t i) -> p c t i", c=1, i=1).to_broadcast([P, H // LINE, PACK, LINE])
+        factor = neg_fk.rearrange("p (c t i) -> p c t i", c=1, i=1).to_broadcast([P, H // LINE, PACK, LINE])
         u_bf, u_w, u_s = [], [], []
         for h in range(HALVES):
             u_bf.append(tile([P, H, PACK], BF16, "u_bf%d" % h))
@@ -168,8 +189,7 @@ def tile_list_two_boundedgaps_other_stepgap_rowpeaks_kernel(
                 in0=gap[:, :, h * H : (h + 1) * H].rearrange("p t (c i) -> p c t i", i=LINE),
                 in1=factor, op=ALU.mult,
             )
-        w_dw, w_ds = deal(w_w, w_s, "w", True)
-        rs3 = tile([P, HALVES, N], F32, "rs3")
+        rs3 = tile([P, HALVES, N], F32, "rs3", "xb_g3")
         nc.scalar.activation(out=rs3[:], in_=rs_sb[:], func=ACT.Copy, scale=0.3)
         a_ps = []
         for h in range(HALVES):
@@ -182,6 +202,7 @@ def tile_list_two_boundedgaps_other_stepgap_rowpeaks_kernel(
                     out=a_ps[h][:, t, :], lhsT=w_dw[:, t, :].bitcast(E5M2), lhsT_scale=w_ds[:, t, :],
                     rhs=u_w[h][:].bitcast(E5M2), rhs_scale=u_s[h][:], start=True, stop=True,
                 )
+        make_step(1, "gap")
         hid_bf, p_ps = [], []
         for h in range(HALVES):
             hid_bf.append(tile([P, H, PACK], BF16, "hid_bf%d" % h))

@@ -70,27 +70,31 @@ def tile_list_two_boundedgaps_other_stepgap_rowpeaks_kernel(
                 in_=src[0, 4 * quad : 4 * quad + 4, :].bitcast(I32),
             )
 
-        nc.sync.dma_start(list_o[:], offs3)
         nc.sync.dma_start(list_b[:], offs2)
-        load_words(xo_w, xo_words)
-        for quad in range(4):
-            load_scales(nc.sync, xo_s, xo_scales, quad)
+        nc.sync.dma_start(list_a[:], offs)
         nc.sync.dma_start(out=xb_sb[0][:], in_=xb_rows[0])
-        load_words(w2_w, w2_words)
+        nc.sync.dma_start(out=xa_sb[0][:], in_=xa_rows[0])
+        nc.sync.dma_start(out=hb_sb[:], in_=hb.rearrange("(p t) o -> p (t o)", t=PACK))
+        nc.sync.dma_start(list_o[:], offs3)
+        load_scales(nc.sync, xo_s, xo_scales, 0)
+        load_scales(nc.sync, xo_s, xo_scales, 1)
+        load_scales(nc.sync, xo_s, xo_scales, 2)
+        load_words(xo_w, xo_words)
+        nc.sync.dma_start(out=xb_sb[1][:], in_=xb_rows[1])
         for quad in range(4):
             load_scales(nc.sync, w2_s, w2_scales, quad)
-        nc.sync.dma_start(list_a[:], offs)
-        nc.sync.dma_start(out=xb_sb[1][:], in_=xb_rows[1])
-        nc.sync.dma_start(out=xa_sb[0][:], in_=xa_rows[0])
-        for quad in range(4):
-            load_scales(nc.sync, w_s, w_scales, quad)
         nc.sync.dma_start(out=xa_sb[1][:], in_=xa_rows[1])
+        load_scales(nc.sync, w_s, w_scales, 0)
+        load_words(w2_w, w2_words)
+        load_scales(nc.sync, w_s, w_scales, 1)
+        load_scales(nc.sync, w_s, w_scales, 2)
+        load_scales(nc.sync, w_s, w_scales, 3)
         load_words(w_w, w_words)
         load_words(wb_w, wb_words)
         nc.sync.dma_start(out=rs_sb[:], in_=rs.rearrange("(h p) n -> p h n", p=P))
         for quad in range(4):
             load_scales(nc.sync, wb_s, wb_scales, quad)
-        nc.gpsimd.dma_start(out=hb_sb[:], in_=hb.rearrange("(p t) o -> p (t o)", t=PACK))
+        load_scales(nc.gpsimd, xo_s, xo_scales, 3)
         nc.gpsimd.dma_start(out=fk_sb[:], in_=fk.rearrange("(p t) o -> p (t o)", t=PACK))
 
         def deal_words(words, name, on_scalar, tag=None):
@@ -112,7 +116,7 @@ def tile_list_two_boundedgaps_other_stepgap_rowpeaks_kernel(
             nc.vector.tensor_copy(out=dealt[:], in_=scales[:].rearrange("p (m t) -> p t m", t=PACK))
             return dealt
 
-        xa_g = [tile([P, J], F32, "xa_g%d" % e) for e in range(2)] * 2
+        xa_g = [tile([P, J], F32, "xa_g%d" % t) for t in range(PACK)]
         xb_g = [tile([P, J], F32, "xb_g%d" % t) for t in range(PACK)]
         gap = tile([P, PACK, J], F32, "gap")
 
@@ -133,13 +137,10 @@ def tile_list_two_boundedgaps_other_stepgap_rowpeaks_kernel(
 
         xo_gw = tile([P, J], U32, "xo_gw")
         xo_gs = tile([P, J], U8, "xo_gs")
-        nc.vector.tensor_copy(out=xo_gw[:], in_=xo_w[:].indirect(list_o[:]))
-        nc.vector.tensor_copy(out=xo_gs[:], in_=xo_s[:].indirect(list_o[:]))
-        w2_dw = deal_words(w2_w, "w2_dw", False)
-        w2_ds = deal_scales(w2_s, "w2_ds")
         step = []
         q_ps = [ps.tile([P, PACK, H], F32, name="q_ps%d" % h) for h in range(HALVES)]
-        for h in range(HALVES):
+
+        def multiply_q(h):
             cols = slice(h * H, (h + 1) * H)
             for t in range(PACK):
                 nc.tensor.matmul_mx(
@@ -163,22 +164,27 @@ def tile_list_two_boundedgaps_other_stepgap_rowpeaks_kernel(
         pick_b(0)
         pick_b(1)
         pick_a(0, False)
-        pick_a(1, False)
-        copy_q(0)
-        copy_q(1)
-        neg_fk = tile([P, PACK], F32, "neg_fk", "w2_ds")[:]
-        nc.gpsimd.tensor_scalar(out=neg_fk, in0=fk_sb[:], scalar1=-1.0, scalar2=0.0, op0=ALU.mult, op1=ALU.add)
+        pick_a(1, True)
         plane_gap(0)
         plane_gap(1)
-        w_ds = deal_scales(w_s, "w_ds", "xb_g0")
-        make_step(0, "xb_g1")
+        neg_fk = tile([P, PACK], F32, "neg_fk", "xb_g0")[:]
+        nc.gpsimd.tensor_scalar(out=neg_fk, in0=fk_sb[:], scalar1=-1.0, scalar2=0.0, op0=ALU.mult, op1=ALU.add)
+        nc.vector.tensor_copy(out=xo_gw[:], in_=xo_w[:].indirect(list_o[:]))
+        nc.vector.tensor_copy(out=xo_gs[:], in_=xo_s[:].indirect(list_o[:]))
+        w2_ds = deal_scales(w2_s, "w2_ds")
         pick_b(2)
         pick_b(3)
         pick_a(2, False)
         pick_a(3, True)
         plane_gap(2)
         plane_gap(3)
-        w_dw = deal_words(w_w, "w_dw", True, "xb_g2")
+        w_ds = deal_scales(w_s, "w_ds", "xb_g2")
+        w2_dw = deal_words(w2_w, "w2_dw", True)
+        w_dw = deal_words(w_w, "w_dw", True)
+        multiply_q(0)
+        multiply_q(1)
+        copy_q(0)
+        copy_q(1)
 
         factor = neg_fk.rearrange("p (c t i) -> p c t i", c=1, i=1).to_broadcast([P, H // LINE, PACK, LINE])
         u_bf, u_w, u_s = [], [], []
@@ -189,8 +195,6 @@ def tile_list_two_boundedgaps_other_stepgap_rowpeaks_kernel(
                 in0=gap[:, :, h * H : (h + 1) * H].rearrange("p t (c i) -> p c t i", i=LINE),
                 in1=factor, op=ALU.mult,
             )
-        rs3 = tile([P, HALVES, N], F32, "rs3", "xb_g3")
-        nc.scalar.activation(out=rs3[:], in_=rs_sb[:], func=ACT.Copy, scale=0.3)
         a_ps = []
         for h in range(HALVES):
             u_w.append(tile([P, H], U32, "u_w%d" % h))
@@ -202,7 +206,10 @@ def tile_list_two_boundedgaps_other_stepgap_rowpeaks_kernel(
                     out=a_ps[h][:, t, :], lhsT=w_dw[:, t, :].bitcast(E5M2), lhsT_scale=w_ds[:, t, :],
                     rhs=u_w[h][:].bitcast(E5M2), rhs_scale=u_s[h][:], start=True, stop=True,
                 )
-        make_step(1, "gap")
+        make_step(0, None)
+        make_step(1, None)
+        rs3 = tile([P, HALVES, N], F32, "rs3", "u_bf1")
+        nc.scalar.activation(out=rs3[:], in_=rs_sb[:], func=ACT.Copy, scale=0.3)
         hid_bf, p_ps = [], []
         for h in range(HALVES):
             hid_bf.append(tile([P, H, PACK], BF16, "hid_bf%d" % h))

@@ -20,7 +20,8 @@ P = 128
 PACK = 4
 H = 128
 HALVES = J // H
-LINE = 4
+QUADS = 4
+RUN = 4
 
 
 def tile_list_two_boundedgaps_other_stepgap_rowpeaks_kernel(
@@ -32,14 +33,15 @@ def tile_list_two_boundedgaps_other_stepgap_rowpeaks_kernel(
         sb = ctx.enter_context(tc.tile_pool(name="sb", bufs=1))
         ps = ctx.enter_context(tc.psum_pool(name="ps", bufs=1))
 
-        def tile(shape, dtype, name, tag=None):
-            return sb.tile(shape, dtype, name=name, tag=tag or name, align_bytes=64)
+        def tile(shape, dtype, name, after=None):
+            return sb.tile(shape, dtype, name=name, tag=after or name, align_bytes=64)
 
         list_a = tile([P, J // 16], U16, "list_a")
         list_b = tile([P, J // 16], U16, "list_b")
         list_o = tile([P, J // 16], U16, "list_o")
-        xa_sb = [tile([P, 2, T], F32, "xa_sb%d" % g) for g in range(2)]
-        xb_sb = [tile([P, 2, S], F32, "xb_sb%d" % g) for g in range(2)]
+        xa_pair = tile([P, 2, T], F32, "xa_pair")
+        xa_planes = [xa_pair[:, 0, :], xa_pair[:, 1, :], tile([P, T], F32, "xa_2")[:], tile([P, T], F32, "xa_3")[:]]
+        xb_pairs = [tile([P, 2, S], F32, "xb_pair%d" % g) for g in range(2)]
         hb_sb = tile([P, PACK], F32, "hb_sb")
         fk_sb = tile([P, PACK], F32, "fk_sb")
         xo_w = tile([P, Z], U32, "xo_w")
@@ -47,13 +49,13 @@ def tile_list_two_boundedgaps_other_stepgap_rowpeaks_kernel(
         w_w = tile([P, R], U32, "w_w")
         w2_w = tile([P, R], U32, "w2_w")
         wb_w = tile([P, N], U32, "wb_w")
-        planes = tile([P, 2 * R + N], U8, "planes")
-        w2_s, w_s, wb_s = planes[:, 0:R], planes[:, R : 2 * R], planes[:, 2 * R : 2 * R + N]
+        weight_s = tile([P, 2 * R + N], U8, "weight_s")
+        w2_s, w_s, wb_s = weight_s[:, 0:R], weight_s[:, R : 2 * R], weight_s[:, 2 * R : 2 * R + N]
         rs_sb = tile([P, HALVES, N], F32, "rs_sb")
         q_sb = tile([P, J + 1, PACK], F32, "q_sb")
 
         nc.vector.memset(xo_s[:].bitcast(I32), 0)
-        nc.gpsimd.memset(planes[:].bitcast(I32), 0)
+        nc.gpsimd.memset(weight_s[:].bitcast(I32), 0)
         zeros = tile([P, PACK], F32, "zeros")
         nc.vector.memset(zeros[:], 0.0)
         nc.scalar.activation(out=q_sb[:, 0, :], in_=zeros[:], func=ACT.Copy)
@@ -64,95 +66,127 @@ def tile_list_two_boundedgaps_other_stepgap_rowpeaks_kernel(
         def load_words(dst, src):
             nc.sync.dma_start(out=dst[:].bitcast(I32), in_=src[0].rearrange("p n t -> p (n t)").bitcast(I32))
 
-        def load_scales(queue, dst, src, quad):
-            queue.dma_start(
-                out=dst[32 * quad : 32 * quad + 4, :].bitcast(I32),
-                in_=src[0, 4 * quad : 4 * quad + 4, :].bitcast(I32),
-            )
+        def load_scales(queue, dst, src, quads):
+            for quad in quads:
+                queue.dma_start(
+                    out=dst[32 * quad : 32 * quad + 4, :].bitcast(I32),
+                    in_=src[0, 4 * quad : 4 * quad + 4, :].bitcast(I32),
+                )
 
         nc.sync.dma_start(list_b[:], offs2)
         nc.sync.dma_start(list_a[:], offs)
-        nc.sync.dma_start(out=xb_sb[0][:], in_=xb_rows[0])
-        nc.sync.dma_start(out=xa_sb[0][:], in_=xa_rows[0])
+        nc.sync.dma_start(out=xb_pairs[0][:], in_=xb_rows[0])
+        nc.sync.dma_start(out=xa_pair[:], in_=xa_rows[0])
         nc.sync.dma_start(out=hb_sb[:], in_=hb.rearrange("(p t) o -> p (t o)", t=PACK))
         nc.sync.dma_start(list_o[:], offs3)
-        load_scales(nc.sync, xo_s, xo_scales, 0)
-        load_scales(nc.sync, xo_s, xo_scales, 1)
-        load_scales(nc.sync, xo_s, xo_scales, 2)
+        load_scales(nc.sync, xo_s, xo_scales, range(QUADS - 1))
         load_words(xo_w, xo_words)
-        nc.sync.dma_start(out=xb_sb[1][:], in_=xb_rows[1])
-        for quad in range(4):
-            load_scales(nc.sync, w2_s, w2_scales, quad)
-        nc.sync.dma_start(out=xa_sb[1][:], in_=xa_rows[1])
-        load_scales(nc.sync, w_s, w_scales, 0)
+        nc.sync.dma_start(out=xb_pairs[1][:], in_=xb_rows[1])
+        load_scales(nc.sync, w2_s, w2_scales, range(QUADS))
+        nc.sync.dma_start(out=xa_planes[2], in_=xa_rows[1][:, 0, :])
         load_words(w2_w, w2_words)
-        load_scales(nc.sync, w_s, w_scales, 1)
-        load_scales(nc.sync, w_s, w_scales, 2)
-        load_scales(nc.sync, w_s, w_scales, 3)
+        nc.sync.dma_start(out=xa_planes[3], in_=xa_rows[1][:, 1, :])
+        load_scales(nc.sync, w_s, w_scales, range(QUADS))
         load_words(w_w, w_words)
         load_words(wb_w, wb_words)
         nc.sync.dma_start(out=rs_sb[:], in_=rs.rearrange("(h p) n -> p h n", p=P))
-        for quad in range(4):
-            load_scales(nc.sync, wb_s, wb_scales, quad)
-        load_scales(nc.gpsimd, xo_s, xo_scales, 3)
+        load_scales(nc.sync, wb_s, wb_scales, range(QUADS))
+        load_scales(nc.gpsimd, xo_s, xo_scales, [QUADS - 1])
         nc.gpsimd.dma_start(out=fk_sb[:], in_=fk.rearrange("(p t) o -> p (t o)", t=PACK))
 
-        def deal_words(words, name, on_scalar, tag=None):
-            dealt = tile([P, PACK, P], U32, name, tag)
-            if on_scalar:
-                nc.scalar.copy(
-                    out=dealt[:].rearrange("p t (c i) -> p c t i", i=LINE),
-                    in_=words[:].rearrange("p (c i t) -> p c t i", i=LINE, t=PACK),
-                )
-            else:
-                nc.vector.tensor_copy(
-                    out=dealt[:].bitcast(I32).rearrange("p t (c i) -> p c t i", i=LINE),
-                    in_=words[:].bitcast(I32).rearrange("p (c i t) -> p c t i", i=LINE, t=PACK),
-                )
+        def deal_words(words, name):
+            dealt = tile([P, PACK, P], U32, name)
+            nc.scalar.copy(
+                out=dealt[:].rearrange("p t (c i) -> p c t i", i=RUN),
+                in_=words[:].rearrange("p (c i t) -> p c t i", i=RUN, t=PACK),
+            )
             return dealt
 
-        def deal_scales(scales, name, tag=None):
-            dealt = tile([P, PACK, P], U8, name, tag)
+        def deal_scales(scales, name, after=None):
+            dealt = tile([P, PACK, P], U8, name, after)
             nc.vector.tensor_copy(out=dealt[:], in_=scales[:].rearrange("p (m t) -> p t m", t=PACK))
             return dealt
 
         xa_g = [tile([P, J], F32, "xa_g%d" % t) for t in range(PACK)]
         xb_g = [tile([P, J], F32, "xb_g%d" % t) for t in range(PACK)]
-        gap = tile([P, PACK, J], F32, "gap")
+        neg_gap = tile([P, PACK, J], F32, "neg_gap")
 
         def pick_b(t):
-            nc.scalar.activation(out=xb_g[t][:], in_=xb_sb[t // 2][:, t % 2, :].indirect(list_b[:]), func=ACT.Copy)
+            nc.scalar.activation(out=xb_g[t][:], in_=xb_pairs[t // 2][:, t % 2, :].indirect(list_b[:]), func=ACT.Copy)
 
-        def pick_a(t, on_scalar):
-            if on_scalar:
-                nc.scalar.activation(out=xa_g[t][:], in_=xa_sb[t // 2][:, t % 2, :].indirect(list_a[:]), func=ACT.Copy)
+        def pick_a(t):
+            if t % 2 == 0:
+                nc.vector.tensor_copy(out=xa_g[t][:], in_=xa_planes[t].indirect(list_a[:]))
             else:
-                nc.vector.tensor_copy(out=xa_g[t][:], in_=xa_sb[t // 2][:, t % 2, :].indirect(list_a[:]))
+                nc.scalar.activation(out=xa_g[t][:], in_=xa_planes[t].indirect(list_a[:]), func=ACT.Copy)
 
-        def plane_gap(t):
+        def make_gap(t):
             nc.vector.scalar_tensor_tensor(
-                out=gap[:, t, :], in0=xb_g[t][:], scalar=hb_sb[:, t : t + 1], in1=xa_g[t][:],
+                out=neg_gap[:, t, :], in0=xb_g[t][:], scalar=hb_sb[:, t : t + 1], in1=xa_g[t][:],
                 op0=ALU.min, op1=ALU.subtract,
             )
 
         xo_gw = tile([P, J], U32, "xo_gw")
         xo_gs = tile([P, J], U8, "xo_gs")
-        step = []
         q_ps = [ps.tile([P, PACK, H], F32, name="q_ps%d" % h) for h in range(HALVES)]
 
-        def multiply_q(h):
+        def copy_q(h):
+            nc.scalar.copy(out=q_sb[:, 1 + h * H : 1 + (h + 1) * H, :], in_=q_ps[h][:].rearrange("p t j -> p j t"))
+
+        pick_b(0)
+        pick_b(1)
+        pick_a(0)
+        pick_a(1)
+        make_gap(0)
+        make_gap(1)
+        neg_fk = tile([P, PACK], F32, "neg_fk", after="xb_g0")[:]
+        nc.gpsimd.tensor_scalar(out=neg_fk, in0=fk_sb[:], scalar1=-1.0, scalar2=0.0, op0=ALU.mult, op1=ALU.add)
+        nc.vector.tensor_copy(out=xo_gw[:], in_=xo_w[:].indirect(list_o[:]))
+        nc.vector.tensor_copy(out=xo_gs[:], in_=xo_s[:].indirect(list_o[:]))
+        w2_ds = deal_scales(w2_s, "w2_ds")
+        pick_b(2)
+        pick_b(3)
+        pick_a(2)
+        w2_dw = deal_words(w2_w, "w2_dw")
+        pick_a(3)
+        make_gap(2)
+        make_gap(3)
+        w_ds = deal_scales(w_s, "w_ds", after="xb_g2")
+        for h in range(HALVES):
             cols = slice(h * H, (h + 1) * H)
             for t in range(PACK):
                 nc.tensor.matmul_mx(
                     out=q_ps[h][:, t, :], lhsT=w2_dw[:, t, :].bitcast(E5M2), lhsT_scale=w2_ds[:, t, :],
                     rhs=xo_gw[:, cols].bitcast(E4M3), rhs_scale=xo_gs[:, cols], start=True, stop=True,
                 )
+        copy_q(0)
+        w_dw = deal_words(w_w, "w_dw")
+        copy_q(1)
 
-        def copy_q(h):
-            nc.scalar.copy(out=q_sb[:, 1 + h * H : 1 + (h + 1) * H, :], in_=q_ps[h][:].rearrange("p t j -> p j t"))
+        factor = neg_fk.rearrange("p (c t i) -> p c t i", c=1, i=1).to_broadcast([P, H // RUN, PACK, RUN])
+        u_bf = []
+        for h in range(HALVES):
+            u_bf.append(tile([P, H, PACK], BF16, "u_bf%d" % h))
+            nc.vector.tensor_tensor(
+                out=u_bf[h][:].rearrange("p (c i) t -> p c t i", i=RUN),
+                in0=neg_gap[:, :, h * H : (h + 1) * H].rearrange("p t (c i) -> p c t i", i=RUN),
+                in1=factor, op=ALU.mult,
+            )
+        a_ps = []
+        for h in range(HALVES):
+            u_w = tile([P, H], U32, "u_w%d" % h)
+            u_s = tile([P, H], U8, "u_s%d" % h)
+            nc.vector.quantize_mx(out=u_w[:].bitcast(E5M2), scales=u_s[:], in_=u_bf[h][:].rearrange("p j t -> p (j t)"))
+            a_ps.append(ps.tile([P, PACK, H], F32, name="a_ps%d" % h))
+            for t in range(PACK):
+                nc.tensor.matmul_mx(
+                    out=a_ps[h][:, t, :], lhsT=w_dw[:, t, :].bitcast(E5M2), lhsT_scale=w_ds[:, t, :],
+                    rhs=u_w[:].bitcast(E5M2), rhs_scale=u_s[:], start=True, stop=True,
+                )
 
-        def make_step(h, tag):
-            step.append(tile([P, H * PACK], F32, "step%d" % h, tag))
+        step = []
+        for h in range(HALVES):
+            step.append(tile([P, H * PACK], F32, "step%d" % h))
             nc.vector.scalar_tensor_tensor(
                 out=step[h][:],
                 in0=q_sb[:, h * H : (h + 1) * H, :].rearrange("p j t -> p (j t)"),
@@ -161,62 +195,17 @@ def tile_list_two_boundedgaps_other_stepgap_rowpeaks_kernel(
                 op0=ALU.mult, op1=ALU.add,
             )
 
-        pick_b(0)
-        pick_b(1)
-        pick_a(0, False)
-        pick_a(1, True)
-        plane_gap(0)
-        plane_gap(1)
-        neg_fk = tile([P, PACK], F32, "neg_fk", "xb_g0")[:]
-        nc.gpsimd.tensor_scalar(out=neg_fk, in0=fk_sb[:], scalar1=-1.0, scalar2=0.0, op0=ALU.mult, op1=ALU.add)
-        nc.vector.tensor_copy(out=xo_gw[:], in_=xo_w[:].indirect(list_o[:]))
-        nc.vector.tensor_copy(out=xo_gs[:], in_=xo_s[:].indirect(list_o[:]))
-        w2_ds = deal_scales(w2_s, "w2_ds")
-        pick_b(2)
-        pick_b(3)
-        pick_a(2, False)
-        pick_a(3, True)
-        plane_gap(2)
-        plane_gap(3)
-        w_ds = deal_scales(w_s, "w_ds", "xb_g2")
-        w2_dw = deal_words(w2_w, "w2_dw", True)
-        w_dw = deal_words(w_w, "w_dw", True)
-        multiply_q(0)
-        multiply_q(1)
-        copy_q(0)
-        copy_q(1)
-
-        factor = neg_fk.rearrange("p (c t i) -> p c t i", c=1, i=1).to_broadcast([P, H // LINE, PACK, LINE])
-        u_bf, u_w, u_s = [], [], []
-        for h in range(HALVES):
-            u_bf.append(tile([P, H, PACK], BF16, "u_bf%d" % h))
-            nc.vector.tensor_tensor(
-                out=u_bf[h][:].rearrange("p (c i) t -> p c t i", i=LINE),
-                in0=gap[:, :, h * H : (h + 1) * H].rearrange("p t (c i) -> p c t i", i=LINE),
-                in1=factor, op=ALU.mult,
-            )
-        a_ps = []
-        for h in range(HALVES):
-            u_w.append(tile([P, H], U32, "u_w%d" % h))
-            u_s.append(tile([P, H], U8, "u_s%d" % h))
-            nc.vector.quantize_mx(out=u_w[h][:].bitcast(E5M2), scales=u_s[h][:], in_=u_bf[h][:].rearrange("p j t -> p (j t)"))
-            a_ps.append(ps.tile([P, PACK, H], F32, name="a_ps%d" % h))
-            for t in range(PACK):
-                nc.tensor.matmul_mx(
-                    out=a_ps[h][:, t, :], lhsT=w_dw[:, t, :].bitcast(E5M2), lhsT_scale=w_ds[:, t, :],
-                    rhs=u_w[h][:].bitcast(E5M2), rhs_scale=u_s[h][:], start=True, stop=True,
-                )
-        make_step(0, None)
-        make_step(1, None)
-        rs3 = tile([P, HALVES, N], F32, "rs3", "u_bf1")
+        rs3 = tile([P, HALVES, N], F32, "rs3", after="u_bf1")
         nc.scalar.activation(out=rs3[:], in_=rs_sb[:], func=ACT.Copy, scale=0.3)
-        hid_bf, p_ps = [], []
+
+        hid_bf = []
         for h in range(HALVES):
             hid_bf.append(tile([P, H, PACK], BF16, "hid_bf%d" % h))
             nc.vector.tensor_tensor(
                 out=hid_bf[h][:], in0=a_ps[h][:].rearrange("p t j -> p j t"),
                 in1=step[h][:].rearrange("p (j t) -> p j t", t=PACK), op=ALU.max,
             )
+        p_ps = []
         for h in range(HALVES):
             hid_w = tile([P, H], U32, "hid_w%d" % h)
             hid_s = tile([P, H], U8, "hid_s%d" % h)
@@ -228,15 +217,15 @@ def tile_list_two_boundedgaps_other_stepgap_rowpeaks_kernel(
             )
         for h in range(HALVES):
             size = tile([P, N], F32, "size%d" % h)
-            peak = tile([P, 1], F32, "peak%d" % h)
-            inv = tile([P, 1], F32, "inv%d" % h)
-            res = tile([P, N], F32, "res%d" % h)
+            divisor = tile([P, 1], F32, "divisor%d" % h)
+            inverse = tile([P, 1], F32, "inverse%d" % h)
+            result = tile([P, N], F32, "result%d" % h)
             nc.scalar.activation(out=size[:], in_=p_ps[h][:], func=ACT.Abs)
             nc.vector.tensor_scalar(
-                out=size[:], in0=size[:], scalar1=0.2, scalar2=None, op0=ALU.add, op1=ALU.max, accum_out=peak[:],
+                out=size[:], in0=size[:], scalar1=0.2, scalar2=None, op0=ALU.add, op1=ALU.max, accum_out=divisor[:],
             )
-            nc.vector.reciprocal(out=inv[:], in_=peak[:])
+            nc.vector.reciprocal(out=inverse[:], in_=divisor[:])
             nc.vector.scalar_tensor_tensor(
-                out=res[:], in0=p_ps[h][:], scalar=inv[:], in1=rs3[:, h, :], op0=ALU.mult, op1=ALU.add,
+                out=result[:], in0=p_ps[h][:], scalar=inverse[:], in1=rs3[:, h, :], op0=ALU.mult, op1=ALU.add,
             )
-            nc.sync.dma_start(out=out[h * H : (h + 1) * H, :], in_=res[:])
+            nc.sync.dma_start(out=out[h * H : (h + 1) * H, :], in_=result[:])

from contextlib import ExitStack

import concourse.mybir as mybir

K, T, J, S, R, F, Z, N = 512, 512, 256, 512, 512, 512, 1024, 256
FLOPS = 2 * J * (K * R + F * R + R * N)

F32 = mybir.dt.float32
BF16 = mybir.dt.bfloat16
I32 = mybir.dt.int32
U32 = mybir.dt.uint32
U16 = mybir.dt.uint16
U8 = mybir.dt.uint8
E4M3 = mybir.dt.float8_e4m3fn_x4
E5M2 = mybir.dt.float8_e5m2_x4
ALU = mybir.AluOpType
ACT = mybir.ActivationFunctionType

P = 128
PACK = 4
H = 128
HALVES = J // H
QUADS = 4
RUN = 4


def tile_list_two_boundedgaps_other_stepgap_rowpeaks_kernel(
    tc, xa, xb, hb, fk, w_words, w_scales, xo_words, xo_scales, w2_words, w2_scales,
    wb_words, wb_scales, rs, offs, offs2, offs3, out,
):
    nc = tc.nc
    with ExitStack() as ctx:
        sb = ctx.enter_context(tc.tile_pool(name="sb", bufs=1))
        ps = ctx.enter_context(tc.psum_pool(name="ps", bufs=1))

        def tile(shape, dtype, name, after=None):
            return sb.tile(shape, dtype, name=name, tag=after or name, align_bytes=64)

        list_a = tile([P, J // 16], U16, "list_a")
        list_b = tile([P, J // 16], U16, "list_b")
        list_o = tile([P, J // 16], U16, "list_o")
        xa_pair = tile([P, 2, T], F32, "xa_pair")
        xa_planes = [xa_pair[:, 0, :], xa_pair[:, 1, :], tile([P, T], F32, "xa_2")[:], tile([P, T], F32, "xa_3")[:]]
        xb_pairs = [tile([P, 2, S], F32, "xb_pair%d" % g) for g in range(2)]
        hb_sb = tile([P, PACK], F32, "hb_sb")
        fk_sb = tile([P, PACK], F32, "fk_sb")
        xo_w = tile([P, Z], U32, "xo_w")
        xo_s = tile([P, Z], U8, "xo_s")
        w_w = tile([P, R], U32, "w_w")
        w2_w = tile([P, R], U32, "w2_w")
        wb_w = tile([P, N], U32, "wb_w")
        weight_s = tile([P, 2 * R + N], U8, "weight_s")
        w2_s, w_s, wb_s = weight_s[:, 0:R], weight_s[:, R : 2 * R], weight_s[:, 2 * R : 2 * R + N]
        rs_sb = tile([P, HALVES, N], F32, "rs_sb")
        q_sb = tile([P, J + 1, PACK], F32, "q_sb")

        nc.vector.memset(xo_s[:].bitcast(I32), 0)
        nc.gpsimd.memset(weight_s[:].bitcast(I32), 0)
        zeros = tile([P, PACK], F32, "zeros")
        nc.vector.memset(zeros[:], 0.0)
        nc.scalar.activation(out=q_sb[:, 0, :], in_=zeros[:], func=ACT.Copy)

        xa_rows = xa.rearrange("(p g e) c -> g p e c", g=2, e=2)
        xb_rows = xb.rearrange("(p g e) c -> g p e c", g=2, e=2)

        def load_words(dst, src):
            nc.sync.dma_start(out=dst[:].bitcast(I32), in_=src[0].rearrange("p n t -> p (n t)").bitcast(I32))

        def load_scales(queue, dst, src, quads):
            for quad in quads:
                queue.dma_start(
                    out=dst[32 * quad : 32 * quad + 4, :].bitcast(I32),
                    in_=src[0, 4 * quad : 4 * quad + 4, :].bitcast(I32),
                )

        nc.sync.dma_start(list_b[:], offs2)
        nc.sync.dma_start(list_a[:], offs)
        nc.sync.dma_start(out=xb_pairs[0][:], in_=xb_rows[0])
        nc.sync.dma_start(out=xa_pair[:], in_=xa_rows[0])
        nc.sync.dma_start(out=hb_sb[:], in_=hb.rearrange("(p t) o -> p (t o)", t=PACK))
        nc.sync.dma_start(list_o[:], offs3)
        load_scales(nc.sync, xo_s, xo_scales, range(QUADS - 1))
        load_words(xo_w, xo_words)
        nc.sync.dma_start(out=xb_pairs[1][:], in_=xb_rows[1])
        load_scales(nc.sync, w2_s, w2_scales, range(QUADS))
        nc.sync.dma_start(out=xa_planes[2], in_=xa_rows[1][:, 0, :])
        load_words(w2_w, w2_words)
        nc.sync.dma_start(out=xa_planes[3], in_=xa_rows[1][:, 1, :])
        load_scales(nc.sync, w_s, w_scales, range(QUADS))
        load_words(w_w, w_words)
        load_words(wb_w, wb_words)
        nc.sync.dma_start(out=rs_sb[:], in_=rs.rearrange("(h p) n -> p h n", p=P))
        load_scales(nc.sync, wb_s, wb_scales, range(QUADS))
        load_scales(nc.gpsimd, xo_s, xo_scales, [QUADS - 1])
        nc.gpsimd.dma_start(out=fk_sb[:], in_=fk.rearrange("(p t) o -> p (t o)", t=PACK))

        def deal_words(words, name):
            dealt = tile([P, PACK, P], U32, name)
            nc.scalar.copy(
                out=dealt[:].rearrange("p t (c i) -> p c t i", i=RUN),
                in_=words[:].rearrange("p (c i t) -> p c t i", i=RUN, t=PACK),
            )
            return dealt

        def deal_scales(scales, name, after=None):
            dealt = tile([P, PACK, P], U8, name, after)
            nc.vector.tensor_copy(out=dealt[:], in_=scales[:].rearrange("p (m t) -> p t m", t=PACK))
            return dealt

        xa_g = [tile([P, J], F32, "xa_g%d" % t) for t in range(PACK)]
        xb_g = [tile([P, J], F32, "xb_g%d" % t) for t in range(PACK)]
        neg_gap = tile([P, PACK, J], F32, "neg_gap")

        def pick_b(t):
            nc.scalar.activation(out=xb_g[t][:], in_=xb_pairs[t // 2][:, t % 2, :].indirect(list_b[:]), func=ACT.Copy)

        def pick_a(t):
            if t % 2 == 0:
                nc.vector.tensor_copy(out=xa_g[t][:], in_=xa_planes[t].indirect(list_a[:]))
            else:
                nc.scalar.activation(out=xa_g[t][:], in_=xa_planes[t].indirect(list_a[:]), func=ACT.Copy)

        def make_gap(t):
            nc.vector.scalar_tensor_tensor(
                out=neg_gap[:, t, :], in0=xb_g[t][:], scalar=hb_sb[:, t : t + 1], in1=xa_g[t][:],
                op0=ALU.min, op1=ALU.subtract,
            )

        xo_gw = tile([P, J], U32, "xo_gw")
        xo_gs = tile([P, J], U8, "xo_gs")
        q_ps = [ps.tile([P, PACK, H], F32, name="q_ps%d" % h) for h in range(HALVES)]

        def copy_q(h):
            nc.scalar.copy(out=q_sb[:, 1 + h * H : 1 + (h + 1) * H, :], in_=q_ps[h][:].rearrange("p t j -> p j t"))

        pick_b(0)
        pick_b(1)
        pick_a(0)
        pick_a(1)
        make_gap(0)
        make_gap(1)
        neg_fk = tile([P, PACK], F32, "neg_fk", after="xb_g0")[:]
        nc.gpsimd.tensor_scalar(out=neg_fk, in0=fk_sb[:], scalar1=-1.0, scalar2=0.0, op0=ALU.mult, op1=ALU.add)
        nc.vector.tensor_copy(out=xo_gw[:], in_=xo_w[:].indirect(list_o[:]))
        nc.vector.tensor_copy(out=xo_gs[:], in_=xo_s[:].indirect(list_o[:]))
        w2_ds = deal_scales(w2_s, "w2_ds")
        pick_b(2)
        pick_b(3)
        pick_a(2)
        w2_dw = deal_words(w2_w, "w2_dw")
        pick_a(3)
        make_gap(2)
        make_gap(3)
        w_ds = deal_scales(w_s, "w_ds", after="xb_g2")
        for h in range(HALVES):
            cols = slice(h * H, (h + 1) * H)
            for t in range(PACK):
                nc.tensor.matmul_mx(
                    out=q_ps[h][:, t, :], lhsT=w2_dw[:, t, :].bitcast(E5M2), lhsT_scale=w2_ds[:, t, :],
                    rhs=xo_gw[:, cols].bitcast(E4M3), rhs_scale=xo_gs[:, cols], start=True, stop=True,
                )
        copy_q(0)
        w_dw = deal_words(w_w, "w_dw")
        copy_q(1)

        factor = neg_fk.rearrange("p (c t i) -> p c t i", c=1, i=1).to_broadcast([P, H // RUN, PACK, RUN])
        u_bf = []
        for h in range(HALVES):
            u_bf.append(tile([P, H, PACK], BF16, "u_bf%d" % h))
            nc.vector.tensor_tensor(
                out=u_bf[h][:].rearrange("p (c i) t -> p c t i", i=RUN),
                in0=neg_gap[:, :, h * H : (h + 1) * H].rearrange("p t (c i) -> p c t i", i=RUN),
                in1=factor, op=ALU.mult,
            )
        a_ps = []
        for h in range(HALVES):
            u_w = tile([P, H], U32, "u_w%d" % h)
            u_s = tile([P, H], U8, "u_s%d" % h)
            nc.vector.quantize_mx(out=u_w[:].bitcast(E5M2), scales=u_s[:], in_=u_bf[h][:].rearrange("p j t -> p (j t)"))
            a_ps.append(ps.tile([P, PACK, H], F32, name="a_ps%d" % h))
            for t in range(PACK):
                nc.tensor.matmul_mx(
                    out=a_ps[h][:, t, :], lhsT=w_dw[:, t, :].bitcast(E5M2), lhsT_scale=w_ds[:, t, :],
                    rhs=u_w[:].bitcast(E5M2), rhs_scale=u_s[:], start=True, stop=True,
                )

        step = []
        for h in range(HALVES):
            step.append(tile([P, H * PACK], F32, "step%d" % h))
            nc.vector.scalar_tensor_tensor(
                out=step[h][:],
                in0=q_sb[:, h * H : (h + 1) * H, :].rearrange("p j t -> p (j t)"),
                scalar=-0.6,
                in1=q_sb[:, 1 + h * H : 1 + (h + 1) * H, :].rearrange("p j t -> p (j t)"),
                op0=ALU.mult, op1=ALU.add,
            )

        rs3 = tile([P, HALVES, N], F32, "rs3", after="u_bf1")
        nc.scalar.activation(out=rs3[:], in_=rs_sb[:], func=ACT.Copy, scale=0.3)

        hid_bf = []
        for h in range(HALVES):
            hid_bf.append(tile([P, H, PACK], BF16, "hid_bf%d" % h))
            nc.vector.tensor_tensor(
                out=hid_bf[h][:], in0=a_ps[h][:].rearrange("p t j -> p j t"),
                in1=step[h][:].rearrange("p (j t) -> p j t", t=PACK), op=ALU.max,
            )
        p_ps = []
        for h in range(HALVES):
            hid_w = tile([P, H], U32, "hid_w%d" % h)
            hid_s = tile([P, H], U8, "hid_s%d" % h)
            nc.vector.quantize_mx(out=hid_w[:].bitcast(E5M2), scales=hid_s[:], in_=hid_bf[h][:].rearrange("p j t -> p (j t)"))
            p_ps.append(ps.tile([P, N], F32, name="p_ps%d" % h))
            nc.tensor.matmul_mx(
                out=p_ps[h][:], lhsT=hid_w[:].bitcast(E5M2), lhsT_scale=hid_s[:],
                rhs=wb_w[:].bitcast(E4M3), rhs_scale=wb_s[:], start=True, stop=True,
            )
        for h in range(HALVES):
            size = tile([P, N], F32, "size%d" % h)
            divisor = tile([P, 1], F32, "divisor%d" % h)
            inverse = tile([P, 1], F32, "inverse%d" % h)
            result = tile([P, N], F32, "result%d" % h)
            nc.scalar.activation(out=size[:], in_=p_ps[h][:], func=ACT.Abs)
            nc.vector.tensor_scalar(
                out=size[:], in0=size[:], scalar1=0.2, scalar2=None, op0=ALU.add, op1=ALU.max, accum_out=divisor[:],
            )
            nc.vector.reciprocal(out=inverse[:], in_=divisor[:])
            nc.vector.scalar_tensor_tensor(
                out=result[:], in0=p_ps[h][:], scalar=inverse[:], in1=rs3[:, h, :], op0=ALU.mult, op1=ALU.add,
            )
            nc.sync.dma_start(out=out[h * H : (h + 1) * H, :], in_=result[:])
